import numpy as np, ml_dtypes
CORES = [16,32,48,64,80]
N = 5
C = 128
def setup_inputs(rng):
    x = rng.standard_normal((N, 128, C), dtype=np.float32) * (0.25 + np.abs(rng.standard_normal((N, 1, C), dtype=np.float32)))
    return {"x": x.astype(ml_dtypes.bfloat16)}
def setup_inputs_big(rng):
    d = setup_inputs(rng)
    for k in ("x",): d[k] = (d[k].astype(np.float32) * 1048576.0).astype(d[k].dtype)
    return d
def setup_inputs_small(rng):
    d = setup_inputs(rng)
    for k in ("x",): d[k] = (d[k].astype(np.float32) * (1 / 1048576.0)).astype(d[k].dtype)
    return d
def setup_inputs_apart(rng):
    d = setup_inputs(rng)
    f = (10.0 ** rng.permutation(np.linspace(-1.5, 1.5, N))).astype(np.float32).reshape(N, 1, 1)
    for k in ("x",): d[k] = (d[k].astype(np.float32) * f).astype(d[k].dtype)
    return d
def setup_inputs_mixed(rng):
    d = setup_inputs(rng)
    f = (10.0 ** rng.uniform(-3, 3, (N, 1, C))).astype(np.float32); shape = rng.integers(3, size=(N, 1, C))
    for k in ("x",):
        x = d[k].astype(np.float32)
        m = x.mean(axis=1, keepdims=True); level = m + np.sign(x - m) * np.abs(x - m).mean(axis=1, keepdims=True) * rng.uniform(0.9, 1.1, x.shape).astype(np.float32)
        other = x * np.where(rng.random(x.shape) < 0.016, 100.0, 1.0).astype(np.float32)
        d[k] = (np.where(shape == 1, level, np.where(shape == 2, other, x)) * f).astype(d[k].dtype)
    return d
def reference(x):
    X = x.astype(np.float64); U = X / np.sqrt((X ** 2).sum(axis=1, keepdims=True))
    y = np.full((N, C, N * C), np.nan)
    for r in range(N):
        for s in range(N):
            if s != r: y[r][:, C * s:C * s + C] = U[r].T @ U[s]
    return {"y": y.astype(ml_dtypes.bfloat16)}

@@ -1,0 +1,138 @@
+from concourse.mybir import AluOpType, ActivationFunctionType
+
+N = 5
+C = 128
+W = N * C
+
+SCRATCH = {
+    "xa": ("sbuf", [128, W], "bfloat16"),
+    "sq": ("sbuf", [128, W], "bfloat16"),
+    "ones": ("sbuf", [128, C], "bfloat16"),
+    "ident": ("sbuf", [128, C], "bfloat16"),
+    "rc": ("sbuf", [128, 8], "float32"),
+    "inv": ("sbuf", [128, 1], "float32"),
+    "dg": ("sbuf", [128, W], "bfloat16"),
+    "gt": ("sbuf", [128, W], "bfloat16"),
+    "yb": ("sbuf", [128, W], "bfloat16"),
+}
+for _k in range(1, N):
+    SCRATCH["pg%d" % _k] = ("psum", [128, 512], "float32")
+    SCRATCH["ps%d" % _k] = ("psum", [128, 512], "float32")
+
+SEMAPHORES = ["ld", "one", "idn", "sent", "st", "inv", "sq0", "su0", "rc0"]
+for _k in range(1, N):
+    SEMAPHORES += ["arr%d" % _k, "sq%d" % _k, "su%d" % _k, "rc%d" % _k, "g%d" % _k, "c%d" % _k, "d%d" % _k,
+                   "o%d" % _k, "e%d" % _k]
+
+
+def rank_program(g, core, T, topo):
+    r = T.rank_of(core)
+    if r is None:
+        return
+    S = T.sem
+    AF = ActivationFunctionType
+    n = len(T.cores)
+    R = n - 1
+
+    def col(s):
+        return slice(s * C, (s + 1) * C)
+
+    def src(k):
+        return (r - k) % n
+
+    own = T.xa[:, col(r)]
+
+    g.sync.dma_start(own, T.x[:]).then_inc(S.ld, 16)
+
+    g.vector.memset(T.ones[:], 1.0).then_inc(S.one, 1)
+    g.wait_ge(S.one, 1)
+    g.affine_select(T.ident[:], T.ones[:], [[-1, C]], AluOpType.is_equal, 0.0, 0, 1).then_inc(S.idn, 1)
+    g.wait_ge(S.ld, 16)
+    sent = 0
+    for k in range(1, R + 1):
+        dst = T.cores[(r + k) % n]
+        rid, pid, _se = topo.addr(dst)
+        m = topo.mask(core, dst)
+        g.remote_dma(own, own, S["arr%d" % k], S.sent, pid, rid, m)
+        sent += bin(m).count("1")
+    arrived = {}
+    for k in range(1, R + 1):
+        arrived[k] = bin(topo.mask(T.cores[src(k)], core)).count("1")
+
+    def Sq(k):
+        s = r if k == 0 else src(k)
+        if k == 0:
+            g.scalar.wait_ge(S.ld, 16)
+        else:
+            g.scalar.wait_ge(S["arr%d" % k], arrived[k])
+        g.scalar.activation(T.sq[:, col(s)], T.xa[:, col(s)], AF.Square).then_inc(S["sq%d" % k], 1)
+
+    def ssum(k):
+        return T.ps1[:, 1:2] if k == 0 else T["ps%d" % k][:, 0:1]
+
+    def Su(k):
+        s = r if k == 0 else src(k)
+        g.tensor.wait_ge(S["sq%d" % k], 1)
+        if k == 0:
+            g.tensor.wait_ge(S.one, 1)
+        if k == 1:
+            g.tensor.wait_ge(S.rc0, 1)
+        g.tensor.matmul(ssum(k), T.sq[:, col(s)], T.ones[:, 0:1], True, True).then_inc(S["su%d" % k], 1)
+
+    def Rc(k):
+        g.vector.wait_ge(S["su%d" % k], 1)
+        g.vector.reciprocal(T.rc[:, k:k + 1], ssum(k)).then_inc(S["rc%d" % k], 1)
+
+    def G(k):
+        g.tensor.wait_ge(S["arr%d" % k], arrived[k])
+        g.tensor.matmul(T["pg%d" % k][:, 0:C], T.xa[:, col(src(k))], own, True, True).then_inc(S["g%d" % k], 1)
+
+    def Cp(k):
+        g.vector.wait_ge(S["g%d" % k], 1)
+        g.vector.tensor_copy(T.gt[:, col(src(k))], T["pg%d" % k][:, 0:C]).then_inc(S["c%d" % k], 1)
+
+    def D(k):
+        g.scalar.wait_ge(S["rc%d" % k], 1)
+        g.scalar.activation(T.dg[:, col(src(k))], T.ident[:], AF.Sqrt, scale=T.rc[:, k:k + 1]).then_inc(
+            S["d%d" % k], 1)
+
+    def O(k):
+        g.tensor.wait_ge(S["d%d" % k], 1)
+        g.tensor.wait_ge(S["c%d" % k], 1)
+        g.tensor.matmul(T["pg%d" % k][:, C:2 * C], T.gt[:, col(src(k))], T.dg[:, col(src(k))], True, True).then_inc(
+            S["o%d" % k], 1)
+
+    def E(k):
+        g.vector.wait_ge(S["o%d" % k], 1)
+        if k == 1:
+            g.vector.wait_ge(S.inv, 1)
+        g.vector.tensor_scalar(T.yb[:, col(src(k))], T["pg%d" % k][:, C:2 * C], T.inv[:, 0:1], None,
+                               AluOpType.mult).then_inc(S["e%d" % k], 1)
+
+    def store(k):
+        g.sync.wait_ge(S["e%d" % k], 1)
+        g.sync.dma_start(T.y[:, col(src(k))], T.yb[:, col(src(k))]).then_inc(S.st, 16)
+
+    Sq(0)
+    Su(0)
+    Rc(0)
+    g.scalar.wait_ge(S.rc0, 1)
+    g.scalar.activation(T.inv[:], T.rc[:, 0:1], AF.Sqrt).then_inc(S.inv, 1)
+    g.scalar.wait_ge(S.idn, 1)
+    g.tensor.wait_ge(S.ld, 16)
+
+    for k in range(1, R + 2):
+        if k <= R:
+            Sq(k)
+            G(k)
+            Su(k)
+            Rc(k)
+            Cp(k)
+        if k >= 2:
+            D(k - 1)
+            O(k - 1)
+            E(k - 1)
+            store(k - 1)
+
+    g.wait_ge(S.sent, sent)
+    g.sync.wait_ge(S.st, 16 * R)

@@ -3,6 +3,7 @@ from concourse.mybir import AluOpType, ActivationFunctionType
 N = 5
 C = 128
 W = N * C
+LAG = N - 2
 
 SCRATCH = {
     "xa": ("sbuf", [128, W], "bfloat16"),
@@ -121,18 +122,18 @@ def rank_program(g, core, T, topo):
     g.scalar.wait_ge(S.idn, 1)
     g.tensor.wait_ge(S.ld, 16)
 
-    for k in range(1, R + 2):
+    for k in range(1, R + 1 + LAG):
         if k <= R:
             Sq(k)
             G(k)
             Su(k)
             Rc(k)
             Cp(k)
-        if k >= 2:
-            D(k - 1)
-            O(k - 1)
-            E(k - 1)
-            store(k - 1)
+        if k - LAG >= 1:
+            D(k - LAG)
+            O(k - LAG)
+            E(k - LAG)
+            store(k - LAG)
 
     g.wait_ge(S.sent, sent)
     g.sync.wait_ge(S.st, 16 * R)

@@ -3,11 +3,12 @@ from concourse.mybir import AluOpType, ActivationFunctionType
 N = 5
 C = 128
 W = N * C
-LAG = N - 2
+SW = C + 8
+RAW = 2
 
 SCRATCH = {
-    "xa": ("sbuf", [128, W], "bfloat16"),
-    "sq": ("sbuf", [128, W], "bfloat16"),
+    "xa": ("sbuf", [128, N * SW], "bfloat16"),
+    "sq": ("sbuf", [128, (RAW + 1) * C], "bfloat16"),
     "ones": ("sbuf", [128, C], "bfloat16"),
     "ident": ("sbuf", [128, C], "bfloat16"),
     "rc": ("sbuf", [128, 8], "float32"),
@@ -18,12 +19,16 @@ SCRATCH = {
 }
 for _k in range(1, N):
     SCRATCH["pg%d" % _k] = ("psum", [128, 512], "float32")
+for _k in range(1, RAW + 1):
     SCRATCH["ps%d" % _k] = ("psum", [128, 512], "float32")
 
-SEMAPHORES = ["ld", "one", "idn", "sent", "st", "inv", "sq0", "su0", "rc0"]
+SEMAPHORES = ["ld", "one", "idn", "sent", "st", "inv", "ssb"]
+for _k in range(0, RAW + 1):
+    SEMAPHORES += ["sq%d" % _k, "su%d" % _k]
+for _k in range(0, N):
+    SEMAPHORES += ["rc%d" % _k]
 for _k in range(1, N):
-    SEMAPHORES += ["arr%d" % _k, "sq%d" % _k, "su%d" % _k, "rc%d" % _k, "g%d" % _k, "c%d" % _k, "d%d" % _k,
-                   "o%d" % _k, "e%d" % _k]
+    SEMAPHORES += ["arr%d" % _k, "g%d" % _k, "c%d" % _k, "d%d" % _k, "o%d" % _k, "e%d" % _k]
 
 
 def rank_program(g, core, T, topo):
@@ -32,6 +37,7 @@ def rank_program(g, core, T, topo):
         return
     S = T.sem
     AF = ActivationFunctionType
+    MUL = AluOpType.mult
     n = len(T.cores)
     R = n - 1
 
@@ -41,9 +47,16 @@ def rank_program(g, core, T, topo):
     def src(k):
         return (r - k) % n
 
-    own = T.xa[:, col(r)]
+    def xs(s, lo=0, hi=C):
+        return T.xa[:, s * SW + lo:s * SW + hi]
 
-    g.sync.dma_start(own, T.x[:]).then_inc(S.ld, 16)
+    def engines(a, b):
+        return bin(topo.mask(a, b)).count("1")
+
+    def wait_arr(q, k):
+        q.wait_ge(S["arr%d" % k], engines(T.cores[src(k)], core))
+
+    g.sync.dma_start(xs(r), T.x[:]).then_inc(S.ld, 16)
 
     g.vector.memset(T.ones[:], 1.0).then_inc(S.one, 1)
     g.wait_ge(S.one, 1)
@@ -53,87 +66,67 @@ def rank_program(g, core, T, topo):
     for k in range(1, R + 1):
         dst = T.cores[(r + k) % n]
         rid, pid, _se = topo.addr(dst)
-        m = topo.mask(core, dst)
-        g.remote_dma(own, own, S["arr%d" % k], S.sent, pid, rid, m)
-        sent += bin(m).count("1")
-    arrived = {}
-    for k in range(1, R + 1):
-        arrived[k] = bin(topo.mask(T.cores[src(k)], core)).count("1")
+        if k == RAW + 1:
+            g.wait_ge(S.ssb, 1)
+        piece = xs(r) if k <= RAW else xs(r, 0, C + 1)
+        g.remote_dma(piece, piece, S["arr%d" % k], S.sent, pid, rid, topo.mask(core, dst))
+        sent += engines(core, dst)
 
-    def Sq(k):
-        s = r if k == 0 else src(k)
-        if k == 0:
-            g.scalar.wait_ge(S.ld, 16)
-        else:
-            g.scalar.wait_ge(S["arr%d" % k], arrived[k])
-        g.scalar.activation(T.sq[:, col(s)], T.xa[:, col(s)], AF.Square).then_inc(S["sq%d" % k], 1)
-
-    def ssum(k):
-        return T.ps1[:, 1:2] if k == 0 else T["ps%d" % k][:, 0:1]
-
-    def Su(k):
-        s = r if k == 0 else src(k)
-        g.tensor.wait_ge(S["sq%d" % k], 1)
-        if k == 0:
-            g.tensor.wait_ge(S.one, 1)
-        if k == 1:
-            g.tensor.wait_ge(S.rc0, 1)
-        g.tensor.matmul(ssum(k), T.sq[:, col(s)], T.ones[:, 0:1], True, True).then_inc(S["su%d" % k], 1)
-
-    def Rc(k):
-        g.vector.wait_ge(S["su%d" % k], 1)
-        g.vector.reciprocal(T.rc[:, k:k + 1], ssum(k)).then_inc(S["rc%d" % k], 1)
-
-    def G(k):
-        g.tensor.wait_ge(S["arr%d" % k], arrived[k])
-        g.tensor.matmul(T["pg%d" % k][:, 0:C], T.xa[:, col(src(k))], own, True, True).then_inc(S["g%d" % k], 1)
-
-    def Cp(k):
-        g.vector.wait_ge(S["g%d" % k], 1)
-        g.vector.tensor_copy(T.gt[:, col(src(k))], T["pg%d" % k][:, 0:C]).then_inc(S["c%d" % k], 1)
-
-    def D(k):
-        g.scalar.wait_ge(S["rc%d" % k], 1)
-        g.scalar.activation(T.dg[:, col(src(k))], T.ident[:], AF.Sqrt, scale=T.rc[:, k:k + 1]).then_inc(
-            S["d%d" % k], 1)
-
-    def O(k):
-        g.tensor.wait_ge(S["d%d" % k], 1)
-        g.tensor.wait_ge(S["c%d" % k], 1)
-        g.tensor.matmul(T["pg%d" % k][:, C:2 * C], T.gt[:, col(src(k))], T.dg[:, col(src(k))], True, True).then_inc(
-            S["o%d" % k], 1)
-
-    def E(k):
-        g.vector.wait_ge(S["o%d" % k], 1)
-        if k == 1:
-            g.vector.wait_ge(S.inv, 1)
-        g.vector.tensor_scalar(T.yb[:, col(src(k))], T["pg%d" % k][:, C:2 * C], T.inv[:, 0:1], None,
-                               AluOpType.mult).then_inc(S["e%d" % k], 1)
-
-    def store(k):
-        g.sync.wait_ge(S["e%d" % k], 1)
-        g.sync.dma_start(T.y[:, col(src(k))], T.yb[:, col(src(k))]).then_inc(S.st, 16)
-
-    Sq(0)
-    Su(0)
-    Rc(0)
+    g.scalar.wait_ge(S.ld, 16)
+    g.scalar.activation(T.sq[:, 0:C], xs(r), AF.Square).then_inc(S.sq0, 1)
+    g.tensor.wait_ge(S.sq0, 1)
+    g.tensor.wait_ge(S.one, 1)
+    g.tensor.matmul(T.ps1[:, 1:2], T.sq[:, 0:C], T.ones[:, 0:1], True, True).then_inc(S.su0, 1)
+    g.vector.wait_ge(S.su0, 1)
+    g.vector.tensor_copy(xs(r, C, C + 1), T.ps1[:, 1:2]).then_inc(S.ssb, 1)
+    g.vector.reciprocal(T.rc[:, 0:1], T.ps1[:, 1:2]).then_inc(S.rc0, 1)
     g.scalar.wait_ge(S.rc0, 1)
     g.scalar.activation(T.inv[:], T.rc[:, 0:1], AF.Sqrt).then_inc(S.inv, 1)
     g.scalar.wait_ge(S.idn, 1)
     g.tensor.wait_ge(S.ld, 16)
 
-    for k in range(1, R + 1 + LAG):
-        if k <= R:
-            Sq(k)
-            G(k)
-            Su(k)
-            Rc(k)
-            Cp(k)
-        if k - LAG >= 1:
-            D(k - LAG)
-            O(k - LAG)
-            E(k - LAG)
-            store(k - LAG)
+    def Cp(k):
+        g.vector.wait_ge(S["g%d" % k], 1)
+        g.vector.tensor_copy(T.gt[:, col(src(k))], T["pg%d" % k][:, 0:C]).then_inc(S["c%d" % k], 1)
+
+    for k in range(1, R + 1):
+        wait_arr(g.tensor, k)
+        g.tensor.matmul(T["pg%d" % k][:, 0:C], xs(src(k)), xs(r), True, True).then_inc(S["g%d" % k], 1)
+        if k <= RAW:
+            g.tensor.wait_ge(S["sq%d" % k], 1)
+            if k == 1:
+                g.tensor.wait_ge(S.rc0, 1)
+                g.tensor.wait_ge(S.ssb, 1)
+            g.tensor.matmul(T["ps%d" % k][:, 0:1], T.sq[:, k * C:(k + 1) * C], T.ones[:, 0:1], True, True).then_inc(
+                S["su%d" % k], 1)
+    for k in range(1, RAW + 1):
+        wait_arr(g.vector, k)
+        g.vector.tensor_tensor(T.sq[:, k * C:(k + 1) * C], xs(src(k)), xs(src(k)), MUL).then_inc(S["sq%d" % k], 1)
+    Cp(1)
+    for k in range(1, R + 1):
+        if k <= RAW:
+            g.vector.wait_ge(S["su%d" % k], 1)
+            g.vector.reciprocal(T.rc[:, k:k + 1], T["ps%d" % k][:, 0:1]).then_inc(S["rc%d" % k], 1)
+        else:
+            wait_arr(g.vector, k)
+            g.vector.reciprocal(T.rc[:, k:k + 1], xs(src(k), C, C + 1)).then_inc(S["rc%d" % k], 1)
+    for k in range(2, R + 1):
+        Cp(k)
+
+    g.vector.wait_ge(S.inv, 1)
+    for k in range(1, R + 1):
+        s = src(k)
+        g.scalar.wait_ge(S["rc%d" % k], 1)
+        g.scalar.activation(T.dg[:, col(s)], T.ident[:], AF.Sqrt, scale=T.rc[:, k:k + 1]).then_inc(S["d%d" % k], 1)
+        g.tensor.wait_ge(S["d%d" % k], 1)
+        g.tensor.wait_ge(S["c%d" % k], 1)
+        g.tensor.matmul(T["pg%d" % k][:, C:2 * C], T.gt[:, col(s)], T.dg[:, col(s)], True, True).then_inc(
+            S["o%d" % k], 1)
+        g.vector.wait_ge(S["o%d" % k], 1)
+        g.vector.tensor_scalar(T.yb[:, col(s)], T["pg%d" % k][:, C:2 * C], T.inv[:, 0:1], None, MUL).then_inc(
+            S["e%d" % k], 1)
+        g.sync.wait_ge(S["e%d" % k], 1)
+        g.sync.dma_start(T.y[:, col(s)], T.yb[:, col(s)]).then_inc(S.st, 16)
 
     g.wait_ge(S.sent, sent)
     g.sync.wait_ge(S.st, 16 * R)

@@ -3,30 +3,29 @@ from concourse.mybir import AluOpType, ActivationFunctionType
 N = 5
 C = 128
 W = N * C
-SW = C + 8
-RAW = 2
+X0 = 8
+HC = C // 2
+SW = X0 + C + 8
 
 SCRATCH = {
     "xa": ("sbuf", [128, N * SW], "bfloat16"),
-    "sq": ("sbuf", [128, (RAW + 1) * C], "bfloat16"),
+    "sq": ("sbuf", [128, 2 * C], "bfloat16"),
     "ones": ("sbuf", [128, C], "bfloat16"),
     "ident": ("sbuf", [128, C], "bfloat16"),
     "rc": ("sbuf", [128, 8], "float32"),
-    "inv": ("sbuf", [128, 1], "float32"),
-    "dg": ("sbuf", [128, W], "bfloat16"),
+    "iv": ("sbuf", [128, 8], "float32"),
+    "dg": ("sbuf", [128, 2 * C], "bfloat16"),
     "gt": ("sbuf", [128, W], "bfloat16"),
     "yb": ("sbuf", [128, W], "bfloat16"),
+    "ps0": ("psum", [128, 512], "float32"),
+    "ps1": ("psum", [128, 512], "float32"),
+    "ph": ("psum", [128, 512], "float32"),
 }
 for _k in range(1, N):
     SCRATCH["pg%d" % _k] = ("psum", [128, 512], "float32")
-for _k in range(1, RAW + 1):
-    SCRATCH["ps%d" % _k] = ("psum", [128, 512], "float32")
 
-SEMAPHORES = ["ld", "one", "idn", "sent", "st", "inv", "ssb"]
-for _k in range(0, RAW + 1):
-    SEMAPHORES += ["sq%d" % _k, "su%d" % _k]
-for _k in range(0, N):
-    SEMAPHORES += ["rc%d" % _k]
+SEMAPHORES = ["ld", "one", "idn", "sent", "st", "inv", "ssb", "rcb", "sq0", "su0", "sq1", "su1", "rc0", "rc1", "rc2",
+              "oh"]
 for _k in range(1, N):
     SEMAPHORES += ["arr%d" % _k, "g%d" % _k, "c%d" % _k, "d%d" % _k, "o%d" % _k, "e%d" % _k]
 
@@ -47,8 +46,17 @@ def rank_program(g, core, T, topo):
     def src(k):
         return (r - k) % n
 
-    def xs(s, lo=0, hi=C):
+    def slot(s, lo, hi):
         return T.xa[:, s * SW + lo:s * SW + hi]
+
+    def xs(s):
+        return slot(s, X0, X0 + C)
+
+    def ssc(s):
+        return slot(s, X0 - 1, X0)
+
+    def rcc(s):
+        return slot(s, X0 + C, X0 + C + 1)
 
     def engines(a, b):
         return bin(topo.mask(a, b)).count("1")
@@ -66,9 +74,15 @@ def rank_program(g, core, T, topo):
     for k in range(1, R + 1):
         dst = T.cores[(r + k) % n]
         rid, pid, _se = topo.addr(dst)
-        if k == RAW + 1:
+        if k == 1:
+            piece = xs(r)
+        elif k == 2:
             g.wait_ge(S.ssb, 1)
-        piece = xs(r) if k <= RAW else xs(r, 0, C + 1)
+            piece = slot(r, X0 - 1, X0 + C)
+        else:
+            if k == 3:
+                g.wait_ge(S.rcb, 1)
+            piece = slot(r, X0, X0 + C + 1)
         g.remote_dma(piece, piece, S["arr%d" % k], S.sent, pid, rid, topo.mask(core, dst))
         sent += engines(core, dst)
 
@@ -76,56 +90,81 @@ def rank_program(g, core, T, topo):
     g.scalar.activation(T.sq[:, 0:C], xs(r), AF.Square).then_inc(S.sq0, 1)
     g.tensor.wait_ge(S.sq0, 1)
     g.tensor.wait_ge(S.one, 1)
-    g.tensor.matmul(T.ps1[:, 1:2], T.sq[:, 0:C], T.ones[:, 0:1], True, True).then_inc(S.su0, 1)
+    g.tensor.matmul(T.ps0[:, 0:1], T.sq[:, 0:C], T.ones[:, 0:1], True, True).then_inc(S.su0, 1)
     g.vector.wait_ge(S.su0, 1)
-    g.vector.tensor_copy(xs(r, C, C + 1), T.ps1[:, 1:2]).then_inc(S.ssb, 1)
-    g.vector.reciprocal(T.rc[:, 0:1], T.ps1[:, 1:2]).then_inc(S.rc0, 1)
+    g.vector.tensor_copy(ssc(r), T.ps0[:, 0:1]).then_inc(S.ssb, 1)
+    g.vector.reciprocal(T.rc[:, 0:1], T.ps0[:, 0:1]).then_inc(S.rc0, 1)
+    g.vector.wait_ge(S.rc0, 1)
+    g.vector.tensor_copy(rcc(r), T.rc[:, 0:1]).then_inc(S.rcb, 1)
     g.scalar.wait_ge(S.rc0, 1)
-    g.scalar.activation(T.inv[:], T.rc[:, 0:1], AF.Sqrt).then_inc(S.inv, 1)
+    g.scalar.activation(T.iv[:, 0:1], T.rc[:, 0:1], AF.Sqrt).then_inc(S.inv, 1)
     g.scalar.wait_ge(S.idn, 1)
     g.tensor.wait_ge(S.ld, 16)
+    g.tensor.wait_ge(S.idn, 1)
 
-    def Cp(k):
-        g.vector.wait_ge(S["g%d" % k], 1)
-        g.vector.tensor_copy(T.gt[:, col(src(k))], T["pg%d" % k][:, 0:C]).then_inc(S["c%d" % k], 1)
+    def O(k):
+        g.tensor.wait_ge(S["c%d" % k], 1)
+        if k <= 2:
+            g.tensor.wait_ge(S["d%d" % k], 1)
+            rhs = T.dg[:, (k - 1) * C:k * C]
+        else:
+            rhs = T.ident[:]
+        if k < R:
+            g.tensor.matmul(T["pg%d" % k][:, C:2 * C], T.gt[:, col(src(k))], rhs, True, True).then_inc(
+                S["o%d" % k], 1)
+        else:
+            g.tensor.matmul(T["pg%d" % k][:, C:C + HC], T.gt[:, col(src(k))], T.ident[:, 0:HC], True, True).then_inc(
+                S["o%d" % k], 1)
+            g.tensor.matmul(T.ph[:, 0:HC], T.gt[:, col(src(k))], T.ident[:, HC:C], True, True).then_inc(S.oh, 1)
 
     for k in range(1, R + 1):
         wait_arr(g.tensor, k)
         g.tensor.matmul(T["pg%d" % k][:, 0:C], xs(src(k)), xs(r), True, True).then_inc(S["g%d" % k], 1)
-        if k <= RAW:
-            g.tensor.wait_ge(S["sq%d" % k], 1)
-            if k == 1:
-                g.tensor.wait_ge(S.rc0, 1)
-                g.tensor.wait_ge(S.ssb, 1)
-            g.tensor.matmul(T["ps%d" % k][:, 0:1], T.sq[:, k * C:(k + 1) * C], T.ones[:, 0:1], True, True).then_inc(
-                S["su%d" % k], 1)
-    for k in range(1, RAW + 1):
-        wait_arr(g.vector, k)
-        g.vector.tensor_tensor(T.sq[:, k * C:(k + 1) * C], xs(src(k)), xs(src(k)), MUL).then_inc(S["sq%d" % k], 1)
-    Cp(1)
-    for k in range(1, R + 1):
-        if k <= RAW:
-            g.vector.wait_ge(S["su%d" % k], 1)
-            g.vector.reciprocal(T.rc[:, k:k + 1], T["ps%d" % k][:, 0:1]).then_inc(S["rc%d" % k], 1)
-        else:
-            wait_arr(g.vector, k)
-            g.vector.reciprocal(T.rc[:, k:k + 1], xs(src(k), C, C + 1)).then_inc(S["rc%d" % k], 1)
-    for k in range(2, R + 1):
-        Cp(k)
+        if k == 1:
+            g.tensor.wait_ge(S.sq1, 1)
+            g.tensor.matmul(T.ps1[:, 0:1], T.sq[:, C:2 * C], T.ones[:, 0:1], True, True).then_inc(S.su1, 1)
+    ORDER = (2, 3, 1, 4)
+    for k in ORDER:
+        O(k)
 
+    for k in (3, 2, 4, 1):
+        if k == 1:
+            g.scalar.wait_ge(S.g1, 1)
+            g.scalar.activation(T.gt[:, col(src(1))], T.pg1[:, 0:C], AF.Copy).then_inc(S.c1, 1)
+        if k <= 2:
+            g.scalar.wait_ge(S["rc%d" % k], 1)
+            g.scalar.activation(T.dg[:, (k - 1) * C:k * C], T.ident[:], AF.Sqrt, scale=T.rc[:, k:k + 1]).then_inc(
+                S["d%d" % k], 1)
+        else:
+            wait_arr(g.scalar, k)
+            g.scalar.activation(T.iv[:, k:k + 1], rcc(src(k)), AF.Sqrt).then_inc(S["d%d" % k], 1)
+    g.scalar.wait_ge(S.inv, 1)
+    g.scalar.wait_ge(S.oh, 1)
+    g.scalar.activation(T.yb[:, src(R) * C + HC:(src(R) + 1) * C], T.ph[:, 0:HC], AF.Copy,
+                        scale=T.iv[:, 0:1]).then_inc(S["e%d" % R], 1)
+
+    wait_arr(g.vector, 1)
+    g.vector.tensor_tensor(T.sq[:, C:2 * C], xs(src(1)), xs(src(1)), MUL).then_inc(S.sq1, 1)
+    wait_arr(g.vector, 2)
+    g.vector.reciprocal(T.rc[:, 2:3], ssc(src(2))).then_inc(S.rc2, 1)
+    g.vector.wait_ge(S.su1, 1)
+    g.vector.reciprocal(T.rc[:, 1:2], T.ps1[:, 0:1]).then_inc(S.rc1, 1)
+    for k in range(2, R + 1):
+        g.vector.wait_ge(S["g%d" % k], 1)
+        if k <= 2:
+            g.vector.tensor_copy(T.gt[:, col(src(k))], T["pg%d" % k][:, 0:C]).then_inc(S["c%d" % k], 1)
+        else:
+            g.vector.wait_ge(S["d%d" % k], 1)
+            g.vector.tensor_scalar(T.gt[:, col(src(k))], T["pg%d" % k][:, 0:C], T.iv[:, k:k + 1], None,
+                                   MUL).then_inc(S["c%d" % k], 1)
     g.vector.wait_ge(S.inv, 1)
-    for k in range(1, R + 1):
+    for k in ORDER:
         s = src(k)
-        g.scalar.wait_ge(S["rc%d" % k], 1)
-        g.scalar.activation(T.dg[:, col(s)], T.ident[:], AF.Sqrt, scale=T.rc[:, k:k + 1]).then_inc(S["d%d" % k], 1)
-        g.tensor.wait_ge(S["d%d" % k], 1)
-        g.tensor.wait_ge(S["c%d" % k], 1)
-        g.tensor.matmul(T["pg%d" % k][:, C:2 * C], T.gt[:, col(s)], T.dg[:, col(s)], True, True).then_inc(
-            S["o%d" % k], 1)
+        wd = C if k < R else HC
         g.vector.wait_ge(S["o%d" % k], 1)
-        g.vector.tensor_scalar(T.yb[:, col(s)], T["pg%d" % k][:, C:2 * C], T.inv[:, 0:1], None, MUL).then_inc(
-            S["e%d" % k], 1)
-        g.sync.wait_ge(S["e%d" % k], 1)
+        g.vector.tensor_scalar(T.yb[:, s * C:s * C + wd], T["pg%d" % k][:, C:C + wd], T.iv[:, 0:1], None,
+                               MUL).then_inc(S["e%d" % k], 1)
+        g.sync.wait_ge(S["e%d" % k], 1 if k < R else 2)
         g.sync.dma_start(T.y[:, col(s)], T.yb[:, col(s)]).then_inc(S.st, 16)
 
     g.wait_ge(S.sent, sent)

from concourse.mybir import AluOpType, ActivationFunctionType

N = 5
C = 128
W = N * C
X0 = 8
HC = C // 2
SW = X0 + C + 8

SCRATCH = {
    "xa": ("sbuf", [128, N * SW], "bfloat16"),
    "sq": ("sbuf", [128, 2 * C], "bfloat16"),
    "ones": ("sbuf", [128, C], "bfloat16"),
    "ident": ("sbuf", [128, C], "bfloat16"),
    "rc": ("sbuf", [128, 8], "float32"),
    "iv": ("sbuf", [128, 8], "float32"),
    "dg": ("sbuf", [128, 2 * C], "bfloat16"),
    "gt": ("sbuf", [128, W], "bfloat16"),
    "yb": ("sbuf", [128, W], "bfloat16"),
    "ps0": ("psum", [128, 512], "float32"),
    "ps1": ("psum", [128, 512], "float32"),
    "ph": ("psum", [128, 512], "float32"),
}
for _k in range(1, N):
    SCRATCH["pg%d" % _k] = ("psum", [128, 512], "float32")

SEMAPHORES = ["ld", "one", "idn", "sent", "st", "inv", "ssb", "rcb", "sq0", "su0", "sq1", "su1", "rc0", "rc1", "rc2",
              "oh"]
for _k in range(1, N):
    SEMAPHORES += ["arr%d" % _k, "g%d" % _k, "c%d" % _k, "d%d" % _k, "o%d" % _k, "e%d" % _k]


def rank_program(g, core, T, topo):
    r = T.rank_of(core)
    if r is None:
        return
    S = T.sem
    AF = ActivationFunctionType
    MUL = AluOpType.mult
    n = len(T.cores)
    R = n - 1

    def col(s):
        return slice(s * C, (s + 1) * C)

    def src(k):
        return (r - k) % n

    def slot(s, lo, hi):
        return T.xa[:, s * SW + lo:s * SW + hi]

    def xs(s):
        return slot(s, X0, X0 + C)

    def ssc(s):
        return slot(s, X0 - 1, X0)

    def rcc(s):
        return slot(s, X0 + C, X0 + C + 1)

    def engines(a, b):
        return bin(topo.mask(a, b)).count("1")

    def wait_arr(q, k):
        q.wait_ge(S["arr%d" % k], engines(T.cores[src(k)], core))

    g.sync.dma_start(xs(r), T.x[:]).then_inc(S.ld, 16)

    g.vector.memset(T.ones[:], 1.0).then_inc(S.one, 1)
    g.wait_ge(S.one, 1)
    g.affine_select(T.ident[:], T.ones[:], [[-1, C]], AluOpType.is_equal, 0.0, 0, 1).then_inc(S.idn, 1)
    g.wait_ge(S.ld, 16)
    sent = 0
    for k in range(1, R + 1):
        dst = T.cores[(r + k) % n]
        rid, pid, _se = topo.addr(dst)
        if k == 1:
            piece = xs(r)
        elif k == 2:
            g.wait_ge(S.ssb, 1)
            piece = slot(r, X0 - 1, X0 + C)
        else:
            if k == 3:
                g.wait_ge(S.rcb, 1)
            piece = slot(r, X0, X0 + C + 1)
        g.remote_dma(piece, piece, S["arr%d" % k], S.sent, pid, rid, topo.mask(core, dst))
        sent += engines(core, dst)

    g.scalar.wait_ge(S.ld, 16)
    g.scalar.activation(T.sq[:, 0:C], xs(r), AF.Square).then_inc(S.sq0, 1)
    g.tensor.wait_ge(S.sq0, 1)
    g.tensor.wait_ge(S.one, 1)
    g.tensor.matmul(T.ps0[:, 0:1], T.sq[:, 0:C], T.ones[:, 0:1], True, True).then_inc(S.su0, 1)
    g.vector.wait_ge(S.su0, 1)
    g.vector.tensor_copy(ssc(r), T.ps0[:, 0:1]).then_inc(S.ssb, 1)
    g.vector.reciprocal(T.rc[:, 0:1], T.ps0[:, 0:1]).then_inc(S.rc0, 1)
    g.vector.wait_ge(S.rc0, 1)
    g.vector.tensor_copy(rcc(r), T.rc[:, 0:1]).then_inc(S.rcb, 1)
    g.scalar.wait_ge(S.rc0, 1)
    g.scalar.activation(T.iv[:, 0:1], T.rc[:, 0:1], AF.Sqrt).then_inc(S.inv, 1)
    g.scalar.wait_ge(S.idn, 1)
    g.tensor.wait_ge(S.ld, 16)
    g.tensor.wait_ge(S.idn, 1)

    def O(k):
        g.tensor.wait_ge(S["c%d" % k], 1)
        if k <= 2:
            g.tensor.wait_ge(S["d%d" % k], 1)
            rhs = T.dg[:, (k - 1) * C:k * C]
        else:
            rhs = T.ident[:]
        if k < R:
            g.tensor.matmul(T["pg%d" % k][:, C:2 * C], T.gt[:, col(src(k))], rhs, True, True).then_inc(
                S["o%d" % k], 1)
        else:
            g.tensor.matmul(T["pg%d" % k][:, C:C + HC], T.gt[:, col(src(k))], T.ident[:, 0:HC], True, True).then_inc(
                S["o%d" % k], 1)
            g.tensor.matmul(T.ph[:, 0:HC], T.gt[:, col(src(k))], T.ident[:, HC:C], True, True).then_inc(S.oh, 1)

    for k in range(1, R + 1):
        wait_arr(g.tensor, k)
        g.tensor.matmul(T["pg%d" % k][:, 0:C], xs(src(k)), xs(r), True, True).then_inc(S["g%d" % k], 1)
        if k == 1:
            g.tensor.wait_ge(S.sq1, 1)
            g.tensor.matmul(T.ps1[:, 0:1], T.sq[:, C:2 * C], T.ones[:, 0:1], True, True).then_inc(S.su1, 1)
    ORDER = (2, 3, 1, 4)
    for k in ORDER:
        O(k)

    for k in (3, 2, 4, 1):
        if k == 1:
            g.scalar.wait_ge(S.g1, 1)
            g.scalar.activation(T.gt[:, col(src(1))], T.pg1[:, 0:C], AF.Copy).then_inc(S.c1, 1)
        if k <= 2:
            g.scalar.wait_ge(S["rc%d" % k], 1)
            g.scalar.activation(T.dg[:, (k - 1) * C:k * C], T.ident[:], AF.Sqrt, scale=T.rc[:, k:k + 1]).then_inc(
                S["d%d" % k], 1)
        else:
            wait_arr(g.scalar, k)
            g.scalar.activation(T.iv[:, k:k + 1], rcc(src(k)), AF.Sqrt).then_inc(S["d%d" % k], 1)
    g.scalar.wait_ge(S.inv, 1)
    g.scalar.wait_ge(S.oh, 1)
    g.scalar.activation(T.yb[:, src(R) * C + HC:(src(R) + 1) * C], T.ph[:, 0:HC], AF.Copy,
                        scale=T.iv[:, 0:1]).then_inc(S["e%d" % R], 1)

    wait_arr(g.vector, 1)
    g.vector.tensor_tensor(T.sq[:, C:2 * C], xs(src(1)), xs(src(1)), MUL).then_inc(S.sq1, 1)
    wait_arr(g.vector, 2)
    g.vector.reciprocal(T.rc[:, 2:3], ssc(src(2))).then_inc(S.rc2, 1)
    g.vector.wait_ge(S.su1, 1)
    g.vector.reciprocal(T.rc[:, 1:2], T.ps1[:, 0:1]).then_inc(S.rc1, 1)
    for k in range(2, R + 1):
        g.vector.wait_ge(S["g%d" % k], 1)
        if k <= 2:
            g.vector.tensor_copy(T.gt[:, col(src(k))], T["pg%d" % k][:, 0:C]).then_inc(S["c%d" % k], 1)
        else:
            g.vector.wait_ge(S["d%d" % k], 1)
            g.vector.tensor_scalar(T.gt[:, col(src(k))], T["pg%d" % k][:, 0:C], T.iv[:, k:k + 1], None,
                                   MUL).then_inc(S["c%d" % k], 1)
    g.vector.wait_ge(S.inv, 1)
    for k in ORDER:
        s = src(k)
        wd = C if k < R else HC
        g.vector.wait_ge(S["o%d" % k], 1)
        g.vector.tensor_scalar(T.yb[:, s * C:s * C + wd], T["pg%d" % k][:, C:C + wd], T.iv[:, 0:1], None,
                               MUL).then_inc(S["e%d" % k], 1)
        g.sync.wait_ge(S["e%d" % k], 1 if k < R else 2)
        g.sync.dma_start(T.y[:, col(s)], T.yb[:, col(s)]).then_inc(S.st, 16)

    g.wait_ge(S.sent, sent)
    g.sync.wait_ge(S.st, 16 * R)
